import numpy as np
import ml_dtypes


def mxq(x, axis, fmt="e4m3"):
    dtype, down = {"e4m3": (ml_dtypes.float8_e4m3fn, 7), "e5m2": (ml_dtypes.float8_e5m2, 14)}[fmt]
    v = np.moveaxis(np.asarray(x, np.float32).astype(ml_dtypes.bfloat16).astype(np.float64), axis, -1)
    blocks = v.reshape(v.shape[:-1] + (-1, 32))
    amax = np.abs(blocks).max(-1, keepdims=True)
    byte = np.maximum(np.where(amax > 0, np.frexp(amax)[1] - 1 + 127, 0) - down, 1)
    scale = np.exp2(byte - 127.0)
    codes = (blocks / scale).astype(np.float32).astype(dtype).astype(np.float64)
    return np.moveaxis((codes * scale).reshape(v.shape), -1, axis)


WIDE = False


def mx_kscale(k):
    if not WIDE:
        return np.ones(k)
    levels = np.array([10, -10, 5, -5, 0])
    if k % 512:
        return np.exp2(np.random.permutation(np.resize(levels, k // 32))).repeat(32)
    a = np.empty((k // 512, 16))
    for p in range(k // 512):
        a[p, :8] = np.random.permutation(np.resize(levels, 8))
        for g in range(8):
            far = levels[np.abs(levels - a[p, g]) >= 10]
            a[p, g + 8] = far[np.random.randint(len(far))]
    return np.exp2(a.ravel()).repeat(32)


def f64(x):
    return np.asarray(x).astype(np.float64)


def striped(idx):
    return np.tile(idx.reshape(-1, 16).T, (8, 1)).astype(np.uint16)


def unstriped(offs):
    return offs[:16].T.reshape(-1).astype(np.int64)


def pack_weight(w):
    k, n = w.shape
    w = f64(np.asarray(w, np.float32).astype(ml_dtypes.bfloat16)).reshape(k // 32, 32, n)
    amax = np.abs(w).max(1)
    byte = np.clip(np.where(amax > 0, np.frexp(amax)[1] - 1 + 127 - 7, 1), 1, 254)
    scaled = (w * np.exp2(127.0 - byte)[:, None, :]).reshape(k, n).astype(np.float32)
    words = np.ascontiguousarray(scaled.reshape(k // 512, 128, 4, n).transpose(0, 1, 3, 2)).astype(ml_dtypes.float8_e4m3fn).view(np.uint8)
    return words, np.ascontiguousarray(byte.astype(np.uint8).reshape(k // 512, 16, n))


def unpack_weight(words, scales):
    g, p, n, _ = words.shape
    vals = np.ascontiguousarray(words).view(ml_dtypes.float8_e4m3fn).astype(np.float64) * np.repeat(np.exp2(scales.astype(np.float64) - 127.0), 8, axis=1)[..., None]
    return vals.transpose(0, 1, 3, 2).reshape(g * 512, n)


E2M1 = np.array([0.0, 0.5, 1.0, 1.5, 2.0, 3.0, 4.0, 6.0, -0.0, -0.5, -1.0, -1.5, -2.0, -3.0, -4.0, -6.0])


def pack_fp4(w):
    k, n = w.shape
    w = f64(np.asarray(w, np.float32).astype(ml_dtypes.bfloat16)).reshape(k // 32, 32, n)
    amax = np.abs(w).max(1)
    mant, ex = np.frexp(amax / 6.0)
    byte = np.clip(np.where(amax > 0, np.where(mant > 0.5, ex, ex - 1) + 127, 1), 1, 254)
    scaled = (w * np.exp2(127.0 - byte)[:, None, :]).reshape(k, n).astype(np.float32)
    c = np.ascontiguousarray(scaled.reshape(k // 512, 128, 4, n).transpose(0, 1, 3, 2)).astype(ml_dtypes.float4_e2m1fn).view(np.uint8) & 0xF
    words = (c[..., 0::2] | (c[..., 1::2] << 4)).reshape(k // 512, 128, 2 * n)
    return np.ascontiguousarray(words), np.ascontiguousarray(byte.astype(np.uint8).reshape(k // 512, 16, n))


def unpack_fp4(words, scales):
    g, _, n = scales.shape
    words = np.ascontiguousarray(words).reshape(g, 128, n, 2)
    nib = np.empty((g, 128, n, 4), np.uint8)
    nib[..., 0::2] = words & 0xF
    nib[..., 1::2] = words >> 4
    vals = E2M1[nib] * np.repeat(np.exp2(scales.astype(np.float64) - 127.0), 8, axis=1)[..., None]
    return vals.transpose(0, 1, 3, 2).reshape(g * 512, n)


def planes(y):
    n, m = y.shape
    v = y.astype(np.float32).astype(ml_dtypes.bfloat16).astype(np.float64).reshape(n // 32, 32, m)
    top = np.abs(v).max(1)
    byte = np.clip(np.where(top > 0, np.frexp(top)[1] - 1 + 127 - 7, 1), 1, 254)
    codes = (v * np.exp2(127.0 - byte)[:, None, :]).reshape(n, m).astype(np.float32).astype(ml_dtypes.float8_e4m3fn).view(np.uint8)
    words = codes.reshape(n // 512, 128, 4, m).transpose(0, 1, 3, 2)
    return np.ascontiguousarray(words), np.ascontiguousarray(byte.astype(np.uint8).reshape(n // 512, 16, m))


K, T, S, N, H, U = 1024, 1024, 512, 512, 512, 1024


def setup_inputs():
    n = np.random.standard_normal
    s = mx_kscale(K)[:, None]
    u = mx_kscale(H)
    packed_xT = pack_weight(n((K, T)) * s)
    packed_w1 = pack_fp4(n((K, N)) / np.sqrt(K) / s)
    packed_w2 = pack_fp4(n((H, N)) / np.sqrt(H) / u[:, None])
    return {
        "x_words": packed_xT[0],
        "x_scales": packed_xT[1],
        "w1_words": packed_w1[0],
        "w1_scales": packed_w1[1],
        "unit": (np.random.uniform(0.6, 1.4, (H, 1)) * u[:, None]).astype(np.float32),
        "w2_words": packed_w2[0],
        "w2_scales": packed_w2[1],
        "offs": striped(np.random.permutation(T)[:S]),
        "e1": striped(np.random.permutation(np.concatenate([np.arange(S), np.random.randint(0, S, U - S)]))),
        "e2": striped(np.random.permutation(np.concatenate([np.arange(S), np.random.randint(0, S, U - S)]))),
        "e3": striped(np.random.permutation(np.concatenate([np.arange(S), np.random.randint(0, S, U - S)]))),
    }


def reference(x_words, x_scales, w1_words, w1_scales, unit, w2_words, w2_scales, offs, e1, e2, e3):
    xq = unpack_weight(x_words, x_scales)[:, unstriped(offs)]
    y = unpack_fp4(w1_words, w1_scales).T @ xq
    y1 = y[:, unstriped(e1)]
    y2 = y[:, unstriped(e2)]
    y3 = y[:, unstriped(e3)]
    hid = f64(unit) * ((y1 * y2) / (np.abs(y3) + 0.7))
    out_0 = unpack_fp4(w2_words, w2_scales).T @ mxq(hid, 0, "e4m3")
    return (out_0,) + planes(out_0)

@@ -1,0 +1,252 @@
+from contextlib import ExitStack
+
+import concourse.mybir as mybir
+
+F32 = mybir.dt.float32
+BF16 = mybir.dt.bfloat16
+I32 = mybir.dt.int32
+U32 = mybir.dt.uint32
+U16 = mybir.dt.uint16
+U8 = mybir.dt.uint8
+FP8X4 = mybir.dt.float8_e4m3fn_x4
+FP4X4 = mybir.dt.float4_e2m1fn_x4
+ACT = mybir.ActivationFunctionType
+MULT = mybir.AluOpType.mult
+MAX = mybir.AluOpType.max
+
+P = 128
+PACK = 4
+PASSES = 2
+T = 1024
+S = 512
+U = 1024
+CHUNKS = (128, 256, 256, 256, 128)
+BANK = 512
+
+FLOPS = 2 * 1024 * 512 * 512 + 2 * 512 * 512 * 1024
+
+
+def tile_picked_yspecmx_rat_po_kernel(
+    tc, x_words, x_scales, w1_words, w1_scales, unit, w2_words, w2_scales, offs, e1, e2, e3, out_0, out_1, out_2
+):
+    nc = tc.nc
+    with ExitStack() as ctx:
+        keep = ctx.enter_context(tc.tile_pool(name="keep", bufs=1))
+        ring = ctx.enter_context(tc.tile_pool(name="ring", bufs=2))
+        psum_y = ctx.enter_context(tc.psum_pool(name="psum_y", bufs=1))
+        psum_o = ctx.enter_context(tc.psum_pool(name="psum_o", bufs=2))
+
+        offs_t = keep.tile([P, S // 16], U16, name="offs_t")
+        e1_t = keep.tile([P, U // 16], U16, name="e1_t")
+        e2_t = keep.tile([P, U // 16], U16, name="e2_t")
+        e3_t = keep.tile([P, U // 16], U16, name="e3_t")
+        unit_t = keep.tile([P, PACK], F32, name="unit_t")
+        xw = [keep.tile([P, T], I32, name="xw%d" % o, align_bytes=64) for o in range(PASSES)]
+        xs = keep.tile([P, PASSES, T], U8, name="xs", align_bytes=64)
+        w1w_raw = keep.tile([P, PASSES, 2 * S], U8, name="w1w_raw", align_bytes=64)
+        w1s_raw = keep.tile([P, PASSES, S], U8, name="w1s_raw", align_bytes=64)
+        w2w_raw = keep.tile([P, 2 * S], U8, name="w2w_raw", align_bytes=64)
+        w2s_raw = keep.tile([P, S], U8, name="w2s_raw", align_bytes=64)
+        w1w = keep.tile([P, PASSES, PACK, 2 * P], U8, name="w1w", align_bytes=64)
+        w1s = keep.tile([P, PASSES, PACK, P], U8, name="w1s", align_bytes=64)
+        w2w = keep.tile([P, PACK, 2 * P], U8, name="w2w", align_bytes=64)
+        w2s = keep.tile([P, PACK, P], U8, name="w2s", align_bytes=64)
+        gw = [keep.tile([P, S], U32, name="gw%d" % o, align_bytes=64) for o in range(PASSES)]
+        gs = [keep.tile([P, S], U8, name="gs%d" % o, align_bytes=64) for o in range(PASSES)]
+        y = [keep.tile([P, S], F32, name="y%d" % t, align_bytes=64) for t in range(PACK)]
+        mag = [keep.tile([P, S], F32, name="mag%d" % t, align_bytes=64) for t in range(PACK)]
+        root = [keep.tile([P, S], F32, name="root%d" % t, align_bytes=64) for t in range(PACK)]
+        factor = [keep.tile([P, S], F32, name="factor%d" % t, align_bytes=64) for t in range(PACK)]
+        out_scales = keep.tile([P, U], U8, name="out_scales", align_bytes=64)
+
+        nc.gpsimd.memset(xs[:].rearrange("p o n -> p (o n)").bitcast(I32), 0)
+        nc.vector.memset(w1s_raw[:].rearrange("p o n -> p (o n)").bitcast(I32), 0)
+        nc.vector.memset(w2s_raw[:].bitcast(I32), 0)
+
+        def load_x_words(o):
+            nc.sync.dma_start(xw[o][:], x_words[o].rearrange("p n t -> p (n t)").bitcast(I32))
+
+        nc.sync.dma_start(w1w_raw[:].bitcast(I32), w1_words.rearrange("o p n -> p o n").bitcast(I32))
+        for q in range(4):
+            nc.sync.dma_start(
+                xs[32 * q : 32 * q + 4, :, :].bitcast(I32),
+                x_scales[:, 4 * q : 4 * q + 4, :].rearrange("o r n -> r o n").bitcast(I32),
+            )
+        nc.sync.dma_start(offs_t[:], offs)
+        load_x_words(0)
+        for q in range(4):
+            nc.sync.dma_start(
+                w1s_raw[32 * q : 32 * q + 4, :, :].bitcast(I32),
+                w1_scales[:, 4 * q : 4 * q + 4, :].rearrange("o r n -> r o n").bitcast(I32),
+            )
+        load_x_words(1)
+        nc.sync.dma_start(e1_t[:], e1)
+        nc.sync.dma_start(e2_t[:], e2)
+        nc.sync.dma_start(unit_t[:], unit.rearrange("(p t) c -> p (t c)", t=PACK))
+        nc.sync.dma_start(e3_t[:], e3)
+        nc.sync.dma_start(w2w_raw[:].bitcast(I32), w2_words[0].bitcast(I32))
+        for q in range(4):
+            nc.sync.dma_start(
+                w2s_raw[32 * q : 32 * q + 4, :].bitcast(I32), w2_scales[0, 4 * q : 4 * q + 4, :].bitcast(I32)
+            )
+
+        nc.vector.tensor_copy(
+            w1w[:].bitcast(U16),
+            w1w_raw[:].bitcast(U16).rearrange("p o (m t) -> p o t m", t=PACK),
+        )
+        nc.vector.tensor_copy(gs[0][:], xs[:, 0, :].indirect(offs_t[:]))
+        nc.vector.tensor_copy(gw[0][:], xw[0][:].bitcast(U32).indirect(offs_t[:]))
+        nc.vector.tensor_copy(w1s[:], w1s_raw[:].rearrange("p o (m t) -> p o t m", t=PACK))
+        nc.vector.tensor_copy(gs[1][:], xs[:, 1, :].indirect(offs_t[:]))
+        nc.vector.tensor_copy(gw[1][:], xw[1][:].bitcast(U32).indirect(offs_t[:]))
+
+        y_banks = [psum_y.tile([P, S], F32, name="y_bank%d" % t) for t in range(PACK)]
+        for o in range(PASSES):
+            for t in range(PACK):
+                nc.tensor.matmul_mx(
+                    out=y_banks[t][:],
+                    lhsT=w1w[:, o, t, :].bitcast(FP4X4),
+                    lhsT_scale=w1s[:, o, t, :],
+                    rhs=gw[o][:].bitcast(FP8X4),
+                    rhs_scale=gs[o][:],
+                    start=(o == 0),
+                    stop=(o == PASSES - 1),
+                )
+
+        nc.vector.tensor_copy(
+            w2w[:].bitcast(U16),
+            w2w_raw[:].bitcast(U16).rearrange("p (m t) -> p t m", t=PACK),
+        )
+        nc.vector.tensor_copy(w2s[:], w2s_raw[:].rearrange("p (m t) -> p t m", t=PACK))
+
+        starts = [sum(CHUNKS[:c]) for c in range(len(CHUNKS))]
+        first = {}
+        both = {}
+        third = {}
+        hid_q = {}
+        banks = {}
+        outs = {}
+
+        def cols(c):
+            return slice(starts[c] // 16, (starts[c] + CHUNKS[c]) // 16)
+
+        def fetch_first(c, t):
+            if t == 0:
+                first[c] = ring.tile([P, PACK, CHUNKS[c]], F32, name="first", align_bytes=64)
+            nc.scalar.activation(first[c][:, t, :], y[t][:].indirect(e1_t[:, cols(c)]), ACT.Copy)
+
+        def fetch_second(c, t):
+            if t == 0:
+                both[c] = ring.tile([P, PACK, CHUNKS[c]], F32, name="both", align_bytes=64)
+            nc.vector.tensor_tensor(both[c][:, t, :], y[t][:].indirect(e2_t[:, cols(c)]), first[c][:, t, :], MULT)
+
+        def fetch_third(c, t):
+            if t == 0:
+                third[c] = ring.tile([P, PACK, CHUNKS[c]], F32, name="third", align_bytes=64)
+            nc.scalar.activation(third[c][:, t, :], factor[t][:].indirect(e3_t[:, cols(c)]), ACT.Copy)
+
+        def make_hid(c):
+            n = CHUNKS[c]
+            hid = ring.tile([P, n, PACK], BF16, name="hid", align_bytes=64)
+            nc.vector.tensor_tensor(
+                hid[:].rearrange("p (a i) t -> p a t i", i=4),
+                both[c][:].rearrange("p t (a i) -> p a t i", i=4),
+                third[c][:].rearrange("p t (a i) -> p a t i", i=4),
+                MULT,
+            )
+            hid_q[c] = hid
+
+        def second_product(c):
+            n = CHUNKS[c]
+            codes = ring.tile([P, n], U32, name="hid_codes", align_bytes=64)
+            scales = ring.tile([P, n], U8, name="hid_scales", align_bytes=64)
+            nc.vector.quantize_mx(
+                out=codes[:].bitcast(FP8X4), scales=scales[:], in_=hid_q[c][:].rearrange("p n t -> p (n t)")
+            )
+            per_bank = BANK // n
+            banks[c] = []
+            for b in range(PACK // per_bank):
+                bank = psum_o.tile([P, per_bank, n], F32, name="out_bank%d" % b)
+                for j in range(per_bank):
+                    t = b * per_bank + j
+                    nc.tensor.matmul_mx(
+                        out=bank[:, j, :],
+                        lhsT=w2w[:, t, :].bitcast(FP4X4),
+                        lhsT_scale=w2s[:, t, :],
+                        rhs=codes[:].bitcast(FP8X4),
+                        rhs_scale=scales[:],
+                        start=True,
+                        stop=True,
+                    )
+                banks[c].append(bank)
+
+        def leave_psum(c):
+            n = CHUNKS[c]
+            per_bank = BANK // n
+            res = ring.tile([P, PACK, n], F32, name="res", align_bytes=64)
+            for b, bank in enumerate(banks[c]):
+                nc.scalar.copy(res[:, b * per_bank : (b + 1) * per_bank, :], bank[:])
+            nc.sync.dma_start(
+                out_0[:, starts[c] : starts[c] + n].rearrange("(p t) r -> p t r", t=PACK), res[:]
+            )
+            outs[c] = res
+
+        def round_result(c):
+            n = CHUNKS[c]
+            rounded = ring.tile([P, n, PACK], BF16, name="rounded", align_bytes=64)
+            nc.vector.tensor_copy(
+                rounded[:].rearrange("p (a i) t -> p a t i", i=4),
+                outs[c][:].rearrange("p t (a i) -> p a t i", i=4),
+            )
+            outs[c] = rounded
+
+        def quantise_result(c):
+            n = CHUNKS[c]
+            codes = ring.tile([P, n], I32, name="out_codes", align_bytes=64)
+            nc.vector.quantize_mx(
+                out=codes[:].bitcast(FP8X4),
+                scales=out_scales[:, starts[c] : starts[c] + n],
+                in_=outs[c][:].rearrange("p n t -> p (n t)"),
+            )
+            nc.sync.dma_start(
+                out_1[0, :, starts[c] : starts[c] + n, :].rearrange("p n t -> p (n t)").bitcast(I32), codes[:]
+            )
+
+        for t in range(PACK):
+            nc.vector.tensor_copy(y[t][:], y_banks[t][:])
+        for t in range(PACK):
+            fetch_first(0, t)
+            if t < 2:
+                nc.scalar.activation(mag[t][:], y[t][:], ACT.Abs)
+            else:
+                nc.vector.scalar_tensor_tensor(mag[t][:], y[t][:], -1.0, y[t][:], MULT, MAX)
+            nc.scalar.activation(root[t][:], mag[t][:], ACT.Abs_reciprocal_sqrt, bias=0.7)
+            fetch_second(0, t)
+            nc.vector.scalar_tensor_tensor(factor[t][:], root[t][:], unit_t[:, t : t + 1], root[t][:], MULT, MULT)
+
+        last = len(CHUNKS) - 1
+        for c in range(len(CHUNKS) + 2):
+            if c <= last:
+                for t in range(PACK):
+                    fetch_third(c, t)
+            if c + 1 <= last:
+                for t in range(PACK):
+                    fetch_first(c + 1, t)
+            if c <= last:
+                make_hid(c)
+            if 2 <= c:
+                round_result(c - 2)
+            if c <= last:
+                second_product(c)
+            if 2 <= c:
+                quantise_result(c - 2)
+            if c + 1 <= last:
+                for t in range(PACK):
+                    fetch_second(c + 1, t)
+            if 1 <= c <= last + 1:
+                leave_psum(c - 1)
+
+        for q in range(4):
+            nc.sync.dma_start(
+                out_2[0, 4 * q : 4 * q + 4, :].bitcast(I32), out_scales[32 * q : 32 * q + 4, :].bitcast(I32)
+            )

@@ -20,7 +20,13 @@ PASSES = 2
 T = 1024
 S = 512
 U = 1024
-CHUNKS = (128, 256, 256, 256, 128)
+GROUPS = (384, 384, 256)
+FUSED = (0,)
+UNITS = (384, 384, 128, 128)
+PIECE = 128
+ABS_ON_VECTOR = ()
+COPY_ON_SCALAR = ()
+ROUND_ON_SCALAR = ()
 BANK = 512
 
 FLOPS = 2 * 1024 * 512 * 512 + 2 * 512 * 512 * 1024
@@ -32,9 +38,7 @@ def tile_picked_yspecmx_rat_po_kernel(
     nc = tc.nc
     with ExitStack() as ctx:
         keep = ctx.enter_context(tc.tile_pool(name="keep", bufs=1))
-        ring = ctx.enter_context(tc.tile_pool(name="ring", bufs=2))
-        psum_y = ctx.enter_context(tc.psum_pool(name="psum_y", bufs=1))
-        psum_o = ctx.enter_context(tc.psum_pool(name="psum_o", bufs=2))
+        psum = ctx.enter_context(tc.psum_pool(name="psum", bufs=1))
 
         offs_t = keep.tile([P, S // 16], U16, name="offs_t")
         e1_t = keep.tile([P, U // 16], U16, name="e1_t")
@@ -48,7 +52,7 @@ def tile_picked_yspecmx_rat_po_kernel(
         w2w_raw = keep.tile([P, 2 * S], U8, name="w2w_raw", align_bytes=64)
         w2s_raw = keep.tile([P, S], U8, name="w2s_raw", align_bytes=64)
         w1w = keep.tile([P, PASSES, PACK, 2 * P], U8, name="w1w", align_bytes=64)
-        w1s = keep.tile([P, PASSES, PACK, P], U8, name="w1s", align_bytes=64)
+        w1s_head = keep.tile([P, PASSES, P], U8, name="w1s_head", align_bytes=64)
         w2w = keep.tile([P, PACK, 2 * P], U8, name="w2w", align_bytes=64)
         w2s = keep.tile([P, PACK, P], U8, name="w2s", align_bytes=64)
         gw = [keep.tile([P, S], U32, name="gw%d" % o, align_bytes=64) for o in range(PASSES)]
@@ -62,6 +66,10 @@ def tile_picked_yspecmx_rat_po_kernel(
         nc.gpsimd.memset(xs[:].rearrange("p o n -> p (o n)").bitcast(I32), 0)
         nc.vector.memset(w1s_raw[:].rearrange("p o n -> p (o n)").bitcast(I32), 0)
         nc.vector.memset(w2s_raw[:].bitcast(I32), 0)
+
+        warm = keep.tile([P, 8], F32, name="warm")
+        nc.vector.memset(warm[:, 0:1], 1.0)
+        nc.scalar.activation(warm[:, 4:5], warm[:, 0:1], ACT.Abs_reciprocal_sqrt, bias=0.7)
 
         def load_x_words(o):
             nc.sync.dma_start(xw[o][:], x_words[o].rearrange("p n t -> p (n t)").bitcast(I32))
@@ -95,18 +103,21 @@ def tile_picked_yspecmx_rat_po_kernel(
             w1w_raw[:].bitcast(U16).rearrange("p o (m t) -> p o t m", t=PACK),
         )
         nc.vector.tensor_copy(gs[0][:], xs[:, 0, :].indirect(offs_t[:]))
-        nc.vector.tensor_copy(gw[0][:], xw[0][:].bitcast(U32).indirect(offs_t[:]))
-        nc.vector.tensor_copy(w1s[:], w1s_raw[:].rearrange("p o (m t) -> p o t m", t=PACK))
         nc.vector.tensor_copy(gs[1][:], xs[:, 1, :].indirect(offs_t[:]))
+        nc.vector.tensor_copy(gw[0][:], xw[0][:].bitcast(U32).indirect(offs_t[:]))
+        w1s_dealt = w1s_raw[:].rearrange("p o (m t) -> p o t m", t=PACK)
+        nc.vector.tensor_copy(w1s_head[:], w1s_dealt[:, :, 0, :])
         nc.vector.tensor_copy(gw[1][:], xw[1][:].bitcast(U32).indirect(offs_t[:]))
+        w1s_rest = keep.tile([P, PASSES, PACK - 1, P], U8, name="w1s_rest", tag="xw1", align_bytes=64)
+        nc.vector.tensor_copy(w1s_rest[:], w1s_dealt[:, :, 1:, :])
 
-        y_banks = [psum_y.tile([P, S], F32, name="y_bank%d" % t) for t in range(PACK)]
-        for o in range(PASSES):
-            for t in range(PACK):
+        y_banks = [psum.tile([P, S], F32, name="bank%d" % t) for t in range(PACK)]
+        for t in range(PACK):
+            for o in range(PASSES):
                 nc.tensor.matmul_mx(
                     out=y_banks[t][:],
                     lhsT=w1w[:, o, t, :].bitcast(FP4X4),
-                    lhsT_scale=w1s[:, o, t, :],
+                    lhsT_scale=w1s_head[:, o, :] if t == 0 else w1s_rest[:, o, t - 1, :],
                     rhs=gw[o][:].bitcast(FP8X4),
                     rhs_scale=gs[o][:],
                     start=(o == 0),
@@ -119,132 +130,134 @@ def tile_picked_yspecmx_rat_po_kernel(
         )
         nc.vector.tensor_copy(w2s[:], w2s_raw[:].rearrange("p (m t) -> p t m", t=PACK))
 
-        starts = [sum(CHUNKS[:c]) for c in range(len(CHUNKS))]
-        first = {}
-        both = {}
-        third = {}
-        hid_q = {}
+        group_start = [sum(GROUPS[:g]) for g in range(len(GROUPS))]
+        unit_start = [sum(UNITS[:u]) for u in range(len(UNITS))]
+        first = [keep.tile([P, PACK, n], F32, name="first%d" % g, align_bytes=64) for g, n in enumerate(GROUPS)]
+        both = [keep.tile([P, PACK, n], F32, name="both%d" % g, align_bytes=64) for g, n in enumerate(GROUPS)]
+        third = [keep.tile([P, PACK, n], F32, name="third%d" % g, align_bytes=64) for g, n in enumerate(GROUPS)]
+        hid = [keep.tile([P, n, PACK], BF16, name="hid%d" % g, align_bytes=64) for g, n in enumerate(GROUPS)]
+        hid_codes = [keep.tile([P, n], U32, name="hid_codes%d" % g, align_bytes=64) for g, n in enumerate(GROUPS)]
+        hid_scales = [keep.tile([P, n], U8, name="hid_scales%d" % g, align_bytes=64) for g, n in enumerate(GROUPS)]
+        res = [keep.tile([P, PACK, n], F32, name="res%d" % u, align_bytes=64) for u, n in enumerate(UNITS)]
+        rounded = [keep.tile([P, n, PACK], BF16, name="rounded%d" % u, align_bytes=64) for u, n in enumerate(UNITS)]
+        out_codes = [keep.tile([P, n], I32, name="out_codes%d" % u, align_bytes=64) for u, n in enumerate(UNITS)]
         banks = {}
-        outs = {}
 
-        def cols(c):
-            return slice(starts[c] // 16, (starts[c] + CHUNKS[c]) // 16)
+        def entries(lst, g):
+            return lst[:, group_start[g] // 16 : (group_start[g] + GROUPS[g]) // 16]
 
-        def fetch_first(c, t):
-            if t == 0:
-                first[c] = ring.tile([P, PACK, CHUNKS[c]], F32, name="first", align_bytes=64)
-            nc.scalar.activation(first[c][:, t, :], y[t][:].indirect(e1_t[:, cols(c)]), ACT.Copy)
+        def planes(tile_):
+            return tile_[:].rearrange("p t (a i) -> p a t i", i=4)
 
-        def fetch_second(c, t):
-            if t == 0:
-                both[c] = ring.tile([P, PACK, CHUNKS[c]], F32, name="both", align_bytes=64)
-            nc.vector.tensor_tensor(both[c][:, t, :], y[t][:].indirect(e2_t[:, cols(c)]), first[c][:, t, :], MULT)
+        def words(tile_):
+            return tile_[:].rearrange("p (a i) t -> p a t i", i=4)
 
-        def fetch_third(c, t):
-            if t == 0:
-                third[c] = ring.tile([P, PACK, CHUNKS[c]], F32, name="third", align_bytes=64)
-            nc.scalar.activation(third[c][:, t, :], factor[t][:].indirect(e3_t[:, cols(c)]), ACT.Copy)
+        def fetch_first(g, t):
+            nc.scalar.activation(first[g][:, t, :], y[t][:].indirect(entries(e1_t, g)), ACT.Copy)
 
-        def make_hid(c):
-            n = CHUNKS[c]
-            hid = ring.tile([P, n, PACK], BF16, name="hid", align_bytes=64)
-            nc.vector.tensor_tensor(
-                hid[:].rearrange("p (a i) t -> p a t i", i=4),
-                both[c][:].rearrange("p t (a i) -> p a t i", i=4),
-                third[c][:].rearrange("p t (a i) -> p a t i", i=4),
-                MULT,
-            )
-            hid_q[c] = hid
+        def fetch_second(g, t):
+            nc.vector.tensor_tensor(both[g][:, t, :], y[t][:].indirect(entries(e2_t, g)), first[g][:, t, :], MULT)
 
-        def second_product(c):
-            n = CHUNKS[c]
-            codes = ring.tile([P, n], U32, name="hid_codes", align_bytes=64)
-            scales = ring.tile([P, n], U8, name="hid_scales", align_bytes=64)
+        def fetch_third(g, t):
+            looked_up = factor[t][:].indirect(entries(e3_t, g))
+            if g in FUSED:
+                nc.vector.tensor_tensor(third[g][:, t, :], looked_up, both[g][:, t, :], MULT)
+            else:
+                nc.scalar.activation(third[g][:, t, :], looked_up, ACT.Copy)
+
+        def make_hid(g):
+            if g in FUSED:
+                nc.vector.tensor_copy(words(hid[g]), planes(third[g]))
+            else:
+                nc.vector.tensor_tensor(words(hid[g]), planes(both[g]), planes(third[g]), MULT)
+
+        def second_product(g):
             nc.vector.quantize_mx(
-                out=codes[:].bitcast(FP8X4), scales=scales[:], in_=hid_q[c][:].rearrange("p n t -> p (n t)")
+                out=hid_codes[g][:].bitcast(FP8X4),
+                scales=hid_scales[g][:],
+                in_=hid[g][:].rearrange("p n t -> p (n t)"),
             )
-            per_bank = BANK // n
-            banks[c] = []
-            for b in range(PACK // per_bank):
-                bank = psum_o.tile([P, per_bank, n], F32, name="out_bank%d" % b)
-                for j in range(per_bank):
-                    t = b * per_bank + j
+            for c0 in range(0, GROUPS[g], PIECE):
+                piece = (group_start[g] + c0) // PIECE
+                bank = psum.tile([P, PACK, PIECE], F32, name="bank%d" % ((PACK + piece) % 8))
+                for t in range(PACK):
                     nc.tensor.matmul_mx(
-                        out=bank[:, j, :],
+                        out=bank[:, t, :],
                         lhsT=w2w[:, t, :].bitcast(FP4X4),
                         lhsT_scale=w2s[:, t, :],
-                        rhs=codes[:].bitcast(FP8X4),
-                        rhs_scale=scales[:],
+                        rhs=hid_codes[g][:, c0 : c0 + PIECE].bitcast(FP8X4),
+                        rhs_scale=hid_scales[g][:, c0 : c0 + PIECE],
                         start=True,
                         stop=True,
                     )
-                banks[c].append(bank)
+                banks[piece] = bank
 
-        def leave_psum(c):
-            n = CHUNKS[c]
-            per_bank = BANK // n
-            res = ring.tile([P, PACK, n], F32, name="res", align_bytes=64)
-            for b, bank in enumerate(banks[c]):
-                nc.scalar.copy(res[:, b * per_bank : (b + 1) * per_bank, :], bank[:])
-            nc.sync.dma_start(
-                out_0[:, starts[c] : starts[c] + n].rearrange("(p t) r -> p t r", t=PACK), res[:]
-            )
-            outs[c] = res
+        def units_of(g):
+            return [u for u in range(len(UNITS)) if group_start[g] <= unit_start[u] < group_start[g] + GROUPS[g]]
 
-        def round_result(c):
-            n = CHUNKS[c]
-            rounded = ring.tile([P, n, PACK], BF16, name="rounded", align_bytes=64)
-            nc.vector.tensor_copy(
-                rounded[:].rearrange("p (a i) t -> p a t i", i=4),
-                outs[c][:].rearrange("p t (a i) -> p a t i", i=4),
-            )
-            outs[c] = rounded
+        def columns(u):
+            return slice(unit_start[u], unit_start[u] + UNITS[u])
 
-        def quantise_result(c):
-            n = CHUNKS[c]
-            codes = ring.tile([P, n], I32, name="out_codes", align_bytes=64)
+        def leave_psum(u):
+            for c0 in range(0, UNITS[u], PIECE):
+                nc.scalar.copy(res[u][:, :, c0 : c0 + PIECE], banks[(unit_start[u] + c0) // PIECE][:])
+            nc.sync.dma_start(out_0[:, columns(u)].rearrange("(p t) r -> p t r", t=PACK), res[u][:])
+
+        def round_result(u):
+            if u in ROUND_ON_SCALAR:
+                nc.scalar.copy(words(rounded[u]), planes(res[u]))
+            else:
+                nc.vector.tensor_copy(words(rounded[u]), planes(res[u]))
+
+        def quantise_result(u):
             nc.vector.quantize_mx(
-                out=codes[:].bitcast(FP8X4),
-                scales=out_scales[:, starts[c] : starts[c] + n],
-                in_=outs[c][:].rearrange("p n t -> p (n t)"),
+                out=out_codes[u][:].bitcast(FP8X4),
+                scales=out_scales[:, columns(u)],
+                in_=rounded[u][:].rearrange("p n t -> p (n t)"),
             )
-            nc.sync.dma_start(
-                out_1[0, :, starts[c] : starts[c] + n, :].rearrange("p n t -> p (n t)").bitcast(I32), codes[:]
-            )
+            nc.sync.dma_start(out_1[0, :, columns(u), :].rearrange("p n t -> p (n t)").bitcast(I32), out_codes[u][:])
 
         for t in range(PACK):
-            nc.vector.tensor_copy(y[t][:], y_banks[t][:])
+            if t in COPY_ON_SCALAR:
+                nc.scalar.copy(y[t][:], y_banks[t][:])
+            else:
+                nc.vector.tensor_copy(y[t][:], y_banks[t][:])
         for t in range(PACK):
             fetch_first(0, t)
-            if t < 2:
-                nc.scalar.activation(mag[t][:], y[t][:], ACT.Abs)
-            else:
+            if t in ABS_ON_VECTOR:
                 nc.vector.scalar_tensor_tensor(mag[t][:], y[t][:], -1.0, y[t][:], MULT, MAX)
+            else:
+                nc.scalar.activation(mag[t][:], y[t][:], ACT.Abs)
             nc.scalar.activation(root[t][:], mag[t][:], ACT.Abs_reciprocal_sqrt, bias=0.7)
             fetch_second(0, t)
             nc.vector.scalar_tensor_tensor(factor[t][:], root[t][:], unit_t[:, t : t + 1], root[t][:], MULT, MULT)
+            if 0 in FUSED:
+                fetch_third(0, t)
 
-        last = len(CHUNKS) - 1
-        for c in range(len(CHUNKS) + 2):
-            if c <= last:
+        last = len(GROUPS) - 1
+        for g in range(last + 3):
+            if g <= last and not (g == 0 and 0 in FUSED):
                 for t in range(PACK):
-                    fetch_third(c, t)
-            if c + 1 <= last:
+                    fetch_third(g, t)
+            if 1 <= g <= last + 1:
+                for u in units_of(g - 1):
+                    leave_psum(u)
+            if g + 1 <= last:
                 for t in range(PACK):
-                    fetch_first(c + 1, t)
-            if c <= last:
-                make_hid(c)
-            if 2 <= c:
-                round_result(c - 2)
-            if c <= last:
-                second_product(c)
-            if 2 <= c:
-                quantise_result(c - 2)
-            if c + 1 <= last:
+                    fetch_first(g + 1, t)
+            if g <= last:
+                make_hid(g)
+            if 2 <= g:
+                for u in units_of(g - 2):
+                    round_result(u)
+            if g <= last:
+                second_product(g)
+            if 2 <= g:
+                for u in units_of(g - 2):
+                    quantise_result(u)
+            if g + 1 <= last:
                 for t in range(PACK):
-                    fetch_second(c + 1, t)
-            if 1 <= c <= last + 1:
-                leave_psum(c - 1)
+                    fetch_second(g + 1, t)
 
         for q in range(4):
             nc.sync.dma_start(

@@ -22,11 +22,14 @@ S = 512
 U = 1024
 GROUPS = (384, 384, 256)
 FUSED = (0,)
-UNITS = (384, 384, 128, 128)
+UNITS = (256, 128, 128, 256, 128, 128)
 PIECE = 128
-ABS_ON_VECTOR = ()
-COPY_ON_SCALAR = ()
-ROUND_ON_SCALAR = ()
+WORD_STORES = {768: 0, 1024: 768}
+HEAD = 2
+EVICT_ON_VECTOR = ()
+ABS_ON_VECTOR = (0,)
+COPY_ON_SCALAR = (0, 1,)
+ROUND_ON_SCALAR = (1,)
 BANK = 512
 
 FLOPS = 2 * 1024 * 512 * 512 + 2 * 512 * 512 * 1024
@@ -46,13 +49,13 @@ def tile_picked_yspecmx_rat_po_kernel(
         e3_t = keep.tile([P, U // 16], U16, name="e3_t")
         unit_t = keep.tile([P, PACK], F32, name="unit_t")
         xw = [keep.tile([P, T], I32, name="xw%d" % o, align_bytes=64) for o in range(PASSES)]
-        xs = keep.tile([P, PASSES, T], U8, name="xs", align_bytes=64)
+        xs = keep.tile([P, T], U8, name="xs", align_bytes=64)
         w1w_raw = keep.tile([P, PASSES, 2 * S], U8, name="w1w_raw", align_bytes=64)
         w1s_raw = keep.tile([P, PASSES, S], U8, name="w1s_raw", align_bytes=64)
         w2w_raw = keep.tile([P, 2 * S], U8, name="w2w_raw", align_bytes=64)
         w2s_raw = keep.tile([P, S], U8, name="w2s_raw", align_bytes=64)
         w1w = keep.tile([P, PASSES, PACK, 2 * P], U8, name="w1w", align_bytes=64)
-        w1s_head = keep.tile([P, PASSES, P], U8, name="w1s_head", align_bytes=64)
+        w1s_head = keep.tile([P, PASSES, HEAD, P], U8, name="w1s_head", align_bytes=64)
         w2w = keep.tile([P, PACK, 2 * P], U8, name="w2w", align_bytes=64)
         w2s = keep.tile([P, PACK, P], U8, name="w2s", align_bytes=64)
         gw = [keep.tile([P, S], U32, name="gw%d" % o, align_bytes=64) for o in range(PASSES)]
@@ -63,7 +66,8 @@ def tile_picked_yspecmx_rat_po_kernel(
         factor = [keep.tile([P, S], F32, name="factor%d" % t, align_bytes=64) for t in range(PACK)]
         out_scales = keep.tile([P, U], U8, name="out_scales", align_bytes=64)
 
-        nc.gpsimd.memset(xs[:].rearrange("p o n -> p (o n)").bitcast(I32), 0)
+        nc.gpsimd.memset(xs[:].bitcast(I32), 0)
+        nc.gpsimd.memset(gs[1][:].bitcast(I32), 0)
         nc.vector.memset(w1s_raw[:].rearrange("p o n -> p (o n)").bitcast(I32), 0)
         nc.vector.memset(w2s_raw[:].bitcast(I32), 0)
 
@@ -77,8 +81,7 @@ def tile_picked_yspecmx_rat_po_kernel(
         nc.sync.dma_start(w1w_raw[:].bitcast(I32), w1_words.rearrange("o p n -> p o n").bitcast(I32))
         for q in range(4):
             nc.sync.dma_start(
-                xs[32 * q : 32 * q + 4, :, :].bitcast(I32),
-                x_scales[:, 4 * q : 4 * q + 4, :].rearrange("o r n -> r o n").bitcast(I32),
+                xs[32 * q : 32 * q + 8, :].bitcast(I32), x_scales[:, 4 * q : 4 * q + 4, :].bitcast(I32)
             )
         nc.sync.dma_start(offs_t[:], offs)
         load_x_words(0)
@@ -102,14 +105,17 @@ def tile_picked_yspecmx_rat_po_kernel(
             w1w[:].bitcast(U16),
             w1w_raw[:].bitcast(U16).rearrange("p o (m t) -> p o t m", t=PACK),
         )
-        nc.vector.tensor_copy(gs[0][:], xs[:, 0, :].indirect(offs_t[:]))
-        nc.vector.tensor_copy(gs[1][:], xs[:, 1, :].indirect(offs_t[:]))
+        nc.vector.tensor_copy(gs[0][:], xs[:].indirect(offs_t[:]))
+        for q in range(4):
+            nc.scalar.dma_start(
+                gs[1][32 * q : 32 * q + 4, :].bitcast(I32), gs[0][32 * q + 4 : 32 * q + 8, :].bitcast(I32)
+            )
         nc.vector.tensor_copy(gw[0][:], xw[0][:].bitcast(U32).indirect(offs_t[:]))
         w1s_dealt = w1s_raw[:].rearrange("p o (m t) -> p o t m", t=PACK)
-        nc.vector.tensor_copy(w1s_head[:], w1s_dealt[:, :, 0, :])
+        nc.vector.tensor_copy(w1s_head[:], w1s_dealt[:, :, :HEAD, :])
         nc.vector.tensor_copy(gw[1][:], xw[1][:].bitcast(U32).indirect(offs_t[:]))
-        w1s_rest = keep.tile([P, PASSES, PACK - 1, P], U8, name="w1s_rest", tag="xw1", align_bytes=64)
-        nc.vector.tensor_copy(w1s_rest[:], w1s_dealt[:, :, 1:, :])
+        w1s_rest = keep.tile([P, PASSES, PACK - HEAD, P], U8, name="w1s_rest", tag="xw1", align_bytes=64)
+        nc.vector.tensor_copy(w1s_rest[:], w1s_dealt[:, :, HEAD:, :])
 
         y_banks = [psum.tile([P, S], F32, name="bank%d" % t) for t in range(PACK)]
         for t in range(PACK):
@@ -117,7 +123,7 @@ def tile_picked_yspecmx_rat_po_kernel(
                 nc.tensor.matmul_mx(
                     out=y_banks[t][:],
                     lhsT=w1w[:, o, t, :].bitcast(FP4X4),
-                    lhsT_scale=w1s_head[:, o, :] if t == 0 else w1s_rest[:, o, t - 1, :],
+                    lhsT_scale=w1s_head[:, o, t, :] if t < HEAD else w1s_rest[:, o, t - HEAD, :],
                     rhs=gw[o][:].bitcast(FP8X4),
                     rhs_scale=gs[o][:],
                     start=(o == 0),
@@ -134,23 +140,33 @@ def tile_picked_yspecmx_rat_po_kernel(
         unit_start = [sum(UNITS[:u]) for u in range(len(UNITS))]
         first = [keep.tile([P, PACK, n], F32, name="first%d" % g, align_bytes=64) for g, n in enumerate(GROUPS)]
         both = [keep.tile([P, PACK, n], F32, name="both%d" % g, align_bytes=64) for g, n in enumerate(GROUPS)]
-        third = [keep.tile([P, PACK, n], F32, name="third%d" % g, align_bytes=64) for g, n in enumerate(GROUPS)]
-        hid = [keep.tile([P, n, PACK], BF16, name="hid%d" % g, align_bytes=64) for g, n in enumerate(GROUPS)]
-        hid_codes = [keep.tile([P, n], U32, name="hid_codes%d" % g, align_bytes=64) for g, n in enumerate(GROUPS)]
-        hid_scales = [keep.tile([P, n], U8, name="hid_scales%d" % g, align_bytes=64) for g, n in enumerate(GROUPS)]
+        third = {}
+        spans = []
+        for g, n in enumerate(GROUPS):
+            if g in FUSED:
+                spans.append((g, group_start[g], n))
+            else:
+                spans.extend(
+                    (g, unit_start[u], UNITS[u])
+                    for u in range(len(UNITS))
+                    if group_start[g] <= unit_start[u] < group_start[g] + n
+                )
+        hid = [keep.tile([P, n, PACK], BF16, name="hid%d" % s, align_bytes=64) for s, (g, c, n) in enumerate(spans)]
+        hid_codes = [keep.tile([P, n], U32, name="hid_codes%d" % s, align_bytes=64) for s, (g, c, n) in enumerate(spans)]
+        hid_scales = [keep.tile([P, n], U8, name="hid_scales%d" % s, align_bytes=64) for s, (g, c, n) in enumerate(spans)]
         res = [keep.tile([P, PACK, n], F32, name="res%d" % u, align_bytes=64) for u, n in enumerate(UNITS)]
         rounded = [keep.tile([P, n, PACK], BF16, name="rounded%d" % u, align_bytes=64) for u, n in enumerate(UNITS)]
-        out_codes = [keep.tile([P, n], I32, name="out_codes%d" % u, align_bytes=64) for u, n in enumerate(UNITS)]
+        out_codes = keep.tile([P, U], I32, name="out_codes", align_bytes=64)
         banks = {}
 
         def entries(lst, g):
             return lst[:, group_start[g] // 16 : (group_start[g] + GROUPS[g]) // 16]
 
         def planes(tile_):
-            return tile_[:].rearrange("p t (a i) -> p a t i", i=4)
+            return tile_.rearrange("p t (a i) -> p a t i", i=4)
 
         def words(tile_):
-            return tile_[:].rearrange("p (a i) t -> p a t i", i=4)
+            return tile_.rearrange("p (a i) t -> p a t i", i=4)
 
         def fetch_first(g, t):
             nc.scalar.activation(first[g][:, t, :], y[t][:].indirect(entries(e1_t, g)), ACT.Copy)
@@ -160,37 +176,49 @@ def tile_picked_yspecmx_rat_po_kernel(
 
         def fetch_third(g, t):
             looked_up = factor[t][:].indirect(entries(e3_t, g))
+            if t == 0:
+                tag = "hid_codes0" if g == len(GROUPS) - 1 else "third%d" % g
+                third[g] = keep.tile([P, PACK, GROUPS[g]], F32, name="third%d" % g, tag=tag, align_bytes=64)
             if g in FUSED:
                 nc.vector.tensor_tensor(third[g][:, t, :], looked_up, both[g][:, t, :], MULT)
             else:
                 nc.scalar.activation(third[g][:, t, :], looked_up, ACT.Copy)
 
         def make_hid(g):
-            if g in FUSED:
-                nc.vector.tensor_copy(words(hid[g]), planes(third[g]))
-            else:
-                nc.vector.tensor_tensor(words(hid[g]), planes(both[g]), planes(third[g]), MULT)
+            for s, (owner, start, n) in enumerate(spans):
+                if owner != g:
+                    continue
+                c0 = start - group_start[g]
+                if g in FUSED:
+                    nc.vector.tensor_copy(words(hid[s][:]), planes(third[g][:]))
+                else:
+                    nc.vector.tensor_tensor(
+                        words(hid[s][:]), planes(both[g][:, :, c0 : c0 + n]), planes(third[g][:, :, c0 : c0 + n]), MULT
+                    )
 
         def second_product(g):
-            nc.vector.quantize_mx(
-                out=hid_codes[g][:].bitcast(FP8X4),
-                scales=hid_scales[g][:],
-                in_=hid[g][:].rearrange("p n t -> p (n t)"),
-            )
-            for c0 in range(0, GROUPS[g], PIECE):
-                piece = (group_start[g] + c0) // PIECE
-                bank = psum.tile([P, PACK, PIECE], F32, name="bank%d" % ((PACK + piece) % 8))
-                for t in range(PACK):
-                    nc.tensor.matmul_mx(
-                        out=bank[:, t, :],
-                        lhsT=w2w[:, t, :].bitcast(FP4X4),
-                        lhsT_scale=w2s[:, t, :],
-                        rhs=hid_codes[g][:, c0 : c0 + PIECE].bitcast(FP8X4),
-                        rhs_scale=hid_scales[g][:, c0 : c0 + PIECE],
-                        start=True,
-                        stop=True,
-                    )
-                banks[piece] = bank
+            for s, (owner, start, n) in enumerate(spans):
+                if owner != g:
+                    continue
+                nc.vector.quantize_mx(
+                    out=hid_codes[s][:].bitcast(FP8X4),
+                    scales=hid_scales[s][:],
+                    in_=hid[s][:].rearrange("p n t -> p (n t)"),
+                )
+                for c0 in range(0, n, PIECE):
+                    piece = (start + c0) // PIECE
+                    bank = psum.tile([P, PACK, PIECE], F32, name="bank%d" % ((PACK + piece) % 8))
+                    for t in range(PACK):
+                        nc.tensor.matmul_mx(
+                            out=bank[:, t, :],
+                            lhsT=w2w[:, t, :].bitcast(FP4X4),
+                            lhsT_scale=w2s[:, t, :],
+                            rhs=hid_codes[s][:, c0 : c0 + PIECE].bitcast(FP8X4),
+                            rhs_scale=hid_scales[s][:, c0 : c0 + PIECE],
+                            start=True,
+                            stop=True,
+                        )
+                    banks[piece] = bank
 
         def units_of(g):
             return [u for u in range(len(UNITS)) if group_start[g] <= unit_start[u] < group_start[g] + GROUPS[g]]
@@ -200,22 +228,31 @@ def tile_picked_yspecmx_rat_po_kernel(
 
         def leave_psum(u):
             for c0 in range(0, UNITS[u], PIECE):
-                nc.scalar.copy(res[u][:, :, c0 : c0 + PIECE], banks[(unit_start[u] + c0) // PIECE][:])
+                piece = (unit_start[u] + c0) // PIECE
+                if piece in EVICT_ON_VECTOR:
+                    nc.vector.tensor_copy(res[u][:, :, c0 : c0 + PIECE], banks[piece][:])
+                else:
+                    nc.scalar.copy(res[u][:, :, c0 : c0 + PIECE], banks[piece][:])
             nc.sync.dma_start(out_0[:, columns(u)].rearrange("(p t) r -> p t r", t=PACK), res[u][:])
 
         def round_result(u):
             if u in ROUND_ON_SCALAR:
-                nc.scalar.copy(words(rounded[u]), planes(res[u]))
+                for c0 in range(0, UNITS[u], PIECE):
+                    bank = banks[(unit_start[u] + c0) // PIECE]
+                    nc.scalar.copy(rounded[u][:, c0 : c0 + PIECE, :], bank[:].rearrange("p t n -> p n t"))
             else:
-                nc.vector.tensor_copy(words(rounded[u]), planes(res[u]))
+                nc.vector.tensor_copy(words(rounded[u][:]), planes(res[u][:]))
 
         def quantise_result(u):
             nc.vector.quantize_mx(
-                out=out_codes[u][:].bitcast(FP8X4),
+                out=out_codes[:, columns(u)].bitcast(FP8X4),
                 scales=out_scales[:, columns(u)],
                 in_=rounded[u][:].rearrange("p n t -> p (n t)"),
             )
-            nc.sync.dma_start(out_1[0, :, columns(u), :].rearrange("p n t -> p (n t)").bitcast(I32), out_codes[u][:])
+            end = unit_start[u] + UNITS[u]
+            if end in WORD_STORES:
+                cols = slice(WORD_STORES[end], end)
+                nc.sync.dma_start(out_1[0, :, cols, :].rearrange("p n t -> p (n t)").bitcast(I32), out_codes[:, cols])
 
         for t in range(PACK):
             if t in COPY_ON_SCALAR:
@@ -260,6 +297,6 @@ def tile_picked_yspecmx_rat_po_kernel(
                     fetch_second(g + 1, t)
 
         for q in range(4):
-            nc.sync.dma_start(
+            (nc.sync if q % 2 == 0 else nc.scalar).dma_start(
                 out_2[0, 4 * q : 4 * q + 4, :].bitcast(I32), out_scales[32 * q : 32 * q + 4, :].bitcast(I32)
             )

@@ -17,20 +17,19 @@ MAX = mybir.AluOpType.max
 P = 128
 PACK = 4
 PASSES = 2
-T = 1024
-S = 512
-U = 1024
+QUADRANTS = 4
+MATERIALS = 1024
+PICKED = 512
+PIXELS = 1024
+BANKS = 8
+OFFSET = 0.7
+
 GROUPS = (384, 384, 256)
-FUSED = (0,)
-UNITS = (256, 128, 128, 256, 128, 128)
 PIECE = 128
-WORD_STORES = {768: 0, 1024: 768}
-HEAD = 2
-EVICT_ON_VECTOR = ()
-ABS_ON_VECTOR = (0,)
-COPY_ON_SCALAR = (0, 1,)
-ROUND_ON_SCALAR = (1,)
-BANK = 512
+STORE = 256
+EARLY_SETS = 2
+SCALAR_COPIES = 2
+VECTOR_ABS = 1
 
 FLOPS = 2 * 1024 * 512 * 512 + 2 * 512 * 512 * 1024
 
@@ -43,260 +42,246 @@ def tile_picked_yspecmx_rat_po_kernel(
         keep = ctx.enter_context(tc.tile_pool(name="keep", bufs=1))
         psum = ctx.enter_context(tc.psum_pool(name="psum", bufs=1))
 
-        offs_t = keep.tile([P, S // 16], U16, name="offs_t")
-        e1_t = keep.tile([P, U // 16], U16, name="e1_t")
-        e2_t = keep.tile([P, U // 16], U16, name="e2_t")
-        e3_t = keep.tile([P, U // 16], U16, name="e3_t")
-        unit_t = keep.tile([P, PACK], F32, name="unit_t")
-        xw = [keep.tile([P, T], I32, name="xw%d" % o, align_bytes=64) for o in range(PASSES)]
-        xs = keep.tile([P, T], U8, name="xs", align_bytes=64)
-        w1w_raw = keep.tile([P, PASSES, 2 * S], U8, name="w1w_raw", align_bytes=64)
-        w1s_raw = keep.tile([P, PASSES, S], U8, name="w1s_raw", align_bytes=64)
-        w2w_raw = keep.tile([P, 2 * S], U8, name="w2w_raw", align_bytes=64)
-        w2s_raw = keep.tile([P, S], U8, name="w2s_raw", align_bytes=64)
-        w1w = keep.tile([P, PASSES, PACK, 2 * P], U8, name="w1w", align_bytes=64)
-        w1s_head = keep.tile([P, PASSES, HEAD, P], U8, name="w1s_head", align_bytes=64)
-        w2w = keep.tile([P, PACK, 2 * P], U8, name="w2w", align_bytes=64)
-        w2s = keep.tile([P, PACK, P], U8, name="w2s", align_bytes=64)
-        gw = [keep.tile([P, S], U32, name="gw%d" % o, align_bytes=64) for o in range(PASSES)]
-        gs = [keep.tile([P, S], U8, name="gs%d" % o, align_bytes=64) for o in range(PASSES)]
-        y = [keep.tile([P, S], F32, name="y%d" % t, align_bytes=64) for t in range(PACK)]
-        mag = [keep.tile([P, S], F32, name="mag%d" % t, align_bytes=64) for t in range(PACK)]
-        root = [keep.tile([P, S], F32, name="root%d" % t, align_bytes=64) for t in range(PACK)]
-        factor = [keep.tile([P, S], F32, name="factor%d" % t, align_bytes=64) for t in range(PACK)]
-        out_scales = keep.tile([P, U], U8, name="out_scales", align_bytes=64)
+        def sbuf(shape, dtype, name, tag=""):
+            return keep.tile(shape, dtype, name=name, tag=tag, align_bytes=64)
 
-        nc.gpsimd.memset(xs[:].bitcast(I32), 0)
-        nc.gpsimd.memset(gs[1][:].bitcast(I32), 0)
-        nc.vector.memset(w1s_raw[:].rearrange("p o n -> p (o n)").bitcast(I32), 0)
-        nc.vector.memset(w2s_raw[:].bitcast(I32), 0)
+        offs_list = keep.tile([P, PICKED // 16], U16, name="offs_list")
+        e1_list = keep.tile([P, PIXELS // 16], U16, name="e1_list")
+        e2_list = keep.tile([P, PIXELS // 16], U16, name="e2_list")
+        e3_list = keep.tile([P, PIXELS // 16], U16, name="e3_list")
+        x_word_table = [sbuf([P, MATERIALS], I32, "x_word_table%d" % o) for o in range(PASSES)]
+        x_scale_table = sbuf([P, MATERIALS], U8, "x_scale_table")
+        w1_words_raw = sbuf([P, PASSES, 2 * PICKED], U8, "w1_words_raw")
+        w1_scales_raw = sbuf([P, PASSES, PICKED], U8, "w1_scales_raw")
+        w1_word_sets = sbuf([P, PASSES, PACK, 2 * P], U8, "w1_word_sets")
+        w1_scales_early = sbuf([P, PASSES, EARLY_SETS, P], U8, "w1_scales_early")
+        w2_word_sets = sbuf([P, PACK, 2 * P], U8, "w2_word_sets")
+        w2_scale_sets = sbuf([P, PACK, P], U8, "w2_scale_sets")
+        picked_words = [sbuf([P, PICKED], U32, "picked_words%d" % o) for o in range(PASSES)]
+        picked_scales = [sbuf([P, PICKED], U8, "picked_scales%d" % o) for o in range(PASSES)]
+        y = [sbuf([P, PICKED], F32, "y%d" % t) for t in range(PACK)]
+        magnitude = [sbuf([P, PICKED], F32, "magnitude%d" % t) for t in range(PACK)]
+        root = [sbuf([P, PICKED], F32, "root%d" % t) for t in range(PACK)]
+        factor = [sbuf([P, PICKED], F32, "factor%d" % t) for t in range(PACK)]
+        out_codes = sbuf([P, PIXELS], I32, "out_codes")
+        out_scales = sbuf([P, PIXELS], U8, "out_scales")
 
-        warm = keep.tile([P, 8], F32, name="warm")
-        nc.vector.memset(warm[:, 0:1], 1.0)
-        nc.scalar.activation(warm[:, 4:5], warm[:, 0:1], ACT.Abs_reciprocal_sqrt, bias=0.7)
+        nc.gpsimd.memset(x_scale_table[:].bitcast(I32), 0)
+        nc.gpsimd.memset(picked_scales[1][:].bitcast(I32), 0)
+        nc.vector.memset(w1_scales_raw[:].rearrange("p o n -> p (o n)").bitcast(I32), 0)
+
+        warm_up = keep.tile([P, 8], F32, name="warm_up")
+        nc.vector.memset(warm_up[:, 0:1], 1.0)
+        nc.scalar.activation(warm_up[:, 4:5], warm_up[:, 0:1], ACT.Abs_reciprocal_sqrt, bias=OFFSET)
 
         def load_x_words(o):
-            nc.sync.dma_start(xw[o][:], x_words[o].rearrange("p n t -> p (n t)").bitcast(I32))
+            nc.sync.dma_start(x_word_table[o][:], x_words[o].rearrange("p n t -> p (n t)").bitcast(I32))
 
-        nc.sync.dma_start(w1w_raw[:].bitcast(I32), w1_words.rearrange("o p n -> p o n").bitcast(I32))
-        for q in range(4):
+        nc.sync.dma_start(w1_words_raw[:].bitcast(I32), w1_words.rearrange("o p n -> p o n").bitcast(I32))
+        for q in range(QUADRANTS):
             nc.sync.dma_start(
-                xs[32 * q : 32 * q + 8, :].bitcast(I32), x_scales[:, 4 * q : 4 * q + 4, :].bitcast(I32)
+                x_scale_table[32 * q : 32 * q + 4 * PASSES, :].bitcast(I32),
+                x_scales[:, 4 * q : 4 * q + 4, :].bitcast(I32),
             )
-        nc.sync.dma_start(offs_t[:], offs)
+        nc.sync.dma_start(offs_list[:], offs)
         load_x_words(0)
-        for q in range(4):
+        for q in range(QUADRANTS):
             nc.sync.dma_start(
-                w1s_raw[32 * q : 32 * q + 4, :, :].bitcast(I32),
+                w1_scales_raw[32 * q : 32 * q + 4, :, :].bitcast(I32),
                 w1_scales[:, 4 * q : 4 * q + 4, :].rearrange("o r n -> r o n").bitcast(I32),
             )
         load_x_words(1)
-        nc.sync.dma_start(e1_t[:], e1)
-        nc.sync.dma_start(e2_t[:], e2)
-        nc.sync.dma_start(unit_t[:], unit.rearrange("(p t) c -> p (t c)", t=PACK))
-        nc.sync.dma_start(e3_t[:], e3)
-        nc.sync.dma_start(w2w_raw[:].bitcast(I32), w2_words[0].bitcast(I32))
-        for q in range(4):
-            nc.sync.dma_start(
-                w2s_raw[32 * q : 32 * q + 4, :].bitcast(I32), w2_scales[0, 4 * q : 4 * q + 4, :].bitcast(I32)
-            )
+        nc.sync.dma_start(e1_list[:], e1)
+        nc.sync.dma_start(e2_list[:], e2)
+        nc.sync.dma_start(e3_list[:], e3)
 
         nc.vector.tensor_copy(
-            w1w[:].bitcast(U16),
-            w1w_raw[:].bitcast(U16).rearrange("p o (m t) -> p o t m", t=PACK),
+            w1_word_sets[:].bitcast(U16), w1_words_raw[:].bitcast(U16).rearrange("p o (m t) -> p o t m", t=PACK)
         )
-        nc.vector.tensor_copy(gs[0][:], xs[:].indirect(offs_t[:]))
-        for q in range(4):
+        nc.vector.tensor_copy(picked_scales[0][:], x_scale_table[:].indirect(offs_list[:]))
+        for q in range(QUADRANTS):
             nc.scalar.dma_start(
-                gs[1][32 * q : 32 * q + 4, :].bitcast(I32), gs[0][32 * q + 4 : 32 * q + 8, :].bitcast(I32)
+                picked_scales[1][32 * q : 32 * q + 4, :].bitcast(I32),
+                picked_scales[0][32 * q + 4 : 32 * q + 8, :].bitcast(I32),
             )
-        nc.vector.tensor_copy(gw[0][:], xw[0][:].bitcast(U32).indirect(offs_t[:]))
-        w1s_dealt = w1s_raw[:].rearrange("p o (m t) -> p o t m", t=PACK)
-        nc.vector.tensor_copy(w1s_head[:], w1s_dealt[:, :, :HEAD, :])
-        nc.vector.tensor_copy(gw[1][:], xw[1][:].bitcast(U32).indirect(offs_t[:]))
-        w1s_rest = keep.tile([P, PASSES, PACK - HEAD, P], U8, name="w1s_rest", tag="xw1", align_bytes=64)
-        nc.vector.tensor_copy(w1s_rest[:], w1s_dealt[:, :, HEAD:, :])
+        w2_scales_raw = sbuf([P, PICKED], U8, "w2_scales_raw", tag="x_scale_table")
+        nc.gpsimd.memset(w2_scales_raw[:].bitcast(I32), 0)
+        for q in range(QUADRANTS):
+            nc.sync.dma_start(
+                w2_scales_raw[32 * q : 32 * q + 4, :].bitcast(I32), w2_scales[0, 4 * q : 4 * q + 4, :].bitcast(I32)
+            )
+        nc.vector.tensor_copy(picked_words[0][:], x_word_table[0][:].bitcast(U32).indirect(offs_list[:]))
+        w2_words_raw = sbuf([P, 2 * PICKED], U8, "w2_words_raw", tag="x_word_table0")
+        nc.sync.dma_start(w2_words_raw[:].bitcast(I32), w2_words[0].bitcast(I32))
+        w1_scales_dealt = w1_scales_raw[:].rearrange("p o (m t) -> p o t m", t=PACK)
+        nc.vector.tensor_copy(w1_scales_early[:], w1_scales_dealt[:, :, :EARLY_SETS, :])
+        nc.vector.tensor_copy(picked_words[1][:], x_word_table[1][:].bitcast(U32).indirect(offs_list[:]))
+        w1_scales_late = sbuf([P, PASSES, PACK - EARLY_SETS, P], U8, "w1_scales_late", tag="x_word_table1")
+        nc.vector.tensor_copy(w1_scales_late[:], w1_scales_dealt[:, :, EARLY_SETS:, :])
+        unit_rows = sbuf([P, PACK], F32, "unit_rows", tag="w1_scales_raw")
+        nc.sync.dma_start(unit_rows[:], unit.rearrange("(p t) c -> p (t c)", t=PACK))
 
-        y_banks = [psum.tile([P, S], F32, name="bank%d" % t) for t in range(PACK)]
+        y_banks = [psum.tile([P, PICKED], F32, name="bank%d" % t) for t in range(PACK)]
         for t in range(PACK):
             for o in range(PASSES):
                 nc.tensor.matmul_mx(
                     out=y_banks[t][:],
-                    lhsT=w1w[:, o, t, :].bitcast(FP4X4),
-                    lhsT_scale=w1s_head[:, o, t, :] if t < HEAD else w1s_rest[:, o, t - HEAD, :],
-                    rhs=gw[o][:].bitcast(FP8X4),
-                    rhs_scale=gs[o][:],
+                    lhsT=w1_word_sets[:, o, t, :].bitcast(FP4X4),
+                    lhsT_scale=(
+                        w1_scales_early[:, o, t, :] if t < EARLY_SETS else w1_scales_late[:, o, t - EARLY_SETS, :]
+                    ),
+                    rhs=picked_words[o][:].bitcast(FP8X4),
+                    rhs_scale=picked_scales[o][:],
                     start=(o == 0),
                     stop=(o == PASSES - 1),
                 )
 
         nc.vector.tensor_copy(
-            w2w[:].bitcast(U16),
-            w2w_raw[:].bitcast(U16).rearrange("p (m t) -> p t m", t=PACK),
+            w2_word_sets[:].bitcast(U16), w2_words_raw[:].bitcast(U16).rearrange("p (m t) -> p t m", t=PACK)
         )
-        nc.vector.tensor_copy(w2s[:], w2s_raw[:].rearrange("p (m t) -> p t m", t=PACK))
+        nc.vector.tensor_copy(w2_scale_sets[:], w2_scales_raw[:].rearrange("p (m t) -> p t m", t=PACK))
 
-        group_start = [sum(GROUPS[:g]) for g in range(len(GROUPS))]
-        unit_start = [sum(UNITS[:u]) for u in range(len(UNITS))]
-        first = [keep.tile([P, PACK, n], F32, name="first%d" % g, align_bytes=64) for g, n in enumerate(GROUPS)]
-        both = [keep.tile([P, PACK, n], F32, name="both%d" % g, align_bytes=64) for g, n in enumerate(GROUPS)]
+        last = len(GROUPS) - 1
+        groups = [(sum(GROUPS[:g]), sum(GROUPS[: g + 1])) for g in range(len(GROUPS))]
+
+        def cut(start, end, step):
+            edges = [start] + [c for c in range(start + 1, end) if c % step == 0] + [end]
+            return list(zip(edges[:-1], edges[1:]))
+
+        stretches = [cut(start, end, STORE) for start, end in groups[:last]] + [cut(*groups[last], PIECE)]
+        spans = [[groups[0]]] + stretches[1:]
+
+        first = [sbuf([P, PACK, n], F32, "first%d" % g) for g, n in enumerate(GROUPS)]
+        pair = [sbuf([P, PACK, n], F32, "pair%d" % g) for g, n in enumerate(GROUPS)]
         third = {}
-        spans = []
-        for g, n in enumerate(GROUPS):
-            if g in FUSED:
-                spans.append((g, group_start[g], n))
-            else:
-                spans.extend(
-                    (g, unit_start[u], UNITS[u])
-                    for u in range(len(UNITS))
-                    if group_start[g] <= unit_start[u] < group_start[g] + n
-                )
-        hid = [keep.tile([P, n, PACK], BF16, name="hid%d" % s, align_bytes=64) for s, (g, c, n) in enumerate(spans)]
-        hid_codes = [keep.tile([P, n], U32, name="hid_codes%d" % s, align_bytes=64) for s, (g, c, n) in enumerate(spans)]
-        hid_scales = [keep.tile([P, n], U8, name="hid_scales%d" % s, align_bytes=64) for s, (g, c, n) in enumerate(spans)]
-        res = [keep.tile([P, PACK, n], F32, name="res%d" % u, align_bytes=64) for u, n in enumerate(UNITS)]
-        rounded = [keep.tile([P, n, PACK], BF16, name="rounded%d" % u, align_bytes=64) for u, n in enumerate(UNITS)]
-        out_codes = keep.tile([P, U], I32, name="out_codes", align_bytes=64)
-        banks = {}
+        hid = {s: sbuf([P, s[1] - s[0], PACK], BF16, "hid%d" % s[0]) for group in spans for s in group}
+        hid_codes = {s: sbuf([P, s[1] - s[0]], U32, "hid_codes%d" % s[0]) for group in spans for s in group}
+        hid_scales = {s: sbuf([P, s[1] - s[0]], U8, "hid_scales%d" % s[0]) for group in spans for s in group}
+        result = {s: sbuf([P, PACK, s[1] - s[0]], F32, "result%d" % s[0]) for group in stretches for s in group}
+        rounded = {s: sbuf([P, s[1] - s[0], PACK], BF16, "rounded%d" % s[0]) for group in stretches for s in group}
+        out_banks = {}
 
-        def entries(lst, g):
-            return lst[:, group_start[g] // 16 : (group_start[g] + GROUPS[g]) // 16]
+        def entries(index_list, g):
+            return index_list[:, groups[g][0] // 16 : groups[g][1] // 16]
 
-        def planes(tile_):
-            return tile_.rearrange("p t (a i) -> p a t i", i=4)
+        def by_tiles(ap):
+            return ap.rearrange("p t (a i) -> p a t i", i=4)
 
-        def words(tile_):
-            return tile_.rearrange("p (a i) t -> p a t i", i=4)
+        def by_words(ap):
+            return ap.rearrange("p (a i) t -> p a t i", i=4)
 
         def fetch_first(g, t):
-            nc.scalar.activation(first[g][:, t, :], y[t][:].indirect(entries(e1_t, g)), ACT.Copy)
+            nc.scalar.activation(first[g][:, t, :], y[t][:].indirect(entries(e1_list, g)), ACT.Copy)
 
         def fetch_second(g, t):
-            nc.vector.tensor_tensor(both[g][:, t, :], y[t][:].indirect(entries(e2_t, g)), first[g][:, t, :], MULT)
+            nc.vector.tensor_tensor(pair[g][:, t, :], y[t][:].indirect(entries(e2_list, g)), first[g][:, t, :], MULT)
 
         def fetch_third(g, t):
-            looked_up = factor[t][:].indirect(entries(e3_t, g))
             if t == 0:
-                tag = "hid_codes0" if g == len(GROUPS) - 1 else "third%d" % g
-                third[g] = keep.tile([P, PACK, GROUPS[g]], F32, name="third%d" % g, tag=tag, align_bytes=64)
-            if g in FUSED:
-                nc.vector.tensor_tensor(third[g][:, t, :], looked_up, both[g][:, t, :], MULT)
+                tag = "hid_codes0" if g == last else "third%d" % g
+                third[g] = sbuf([P, PACK, GROUPS[g]], F32, "third%d" % g, tag=tag)
+            looked_up = factor[t][:].indirect(entries(e3_list, g))
+            if g == 0:
+                nc.vector.tensor_tensor(third[g][:, t, :], looked_up, pair[g][:, t, :], MULT)
             else:
                 nc.scalar.activation(third[g][:, t, :], looked_up, ACT.Copy)
 
-        def make_hid(g):
-            for s, (owner, start, n) in enumerate(spans):
-                if owner != g:
-                    continue
-                c0 = start - group_start[g]
-                if g in FUSED:
-                    nc.vector.tensor_copy(words(hid[s][:]), planes(third[g][:]))
+        def round_hid(g):
+            for s in spans[g]:
+                if g == 0:
+                    nc.vector.tensor_copy(by_words(hid[s][:]), by_tiles(third[g][:]))
                 else:
+                    cols = slice(s[0] - groups[g][0], s[1] - groups[g][0])
                     nc.vector.tensor_tensor(
-                        words(hid[s][:]), planes(both[g][:, :, c0 : c0 + n]), planes(third[g][:, :, c0 : c0 + n]), MULT
+                        by_words(hid[s][:]), by_tiles(pair[g][:, :, cols]), by_tiles(third[g][:, :, cols]), MULT
                     )
 
         def second_product(g):
-            for s, (owner, start, n) in enumerate(spans):
-                if owner != g:
-                    continue
+            for s in spans[g]:
                 nc.vector.quantize_mx(
                     out=hid_codes[s][:].bitcast(FP8X4),
                     scales=hid_scales[s][:],
                     in_=hid[s][:].rearrange("p n t -> p (n t)"),
                 )
-                for c0 in range(0, n, PIECE):
-                    piece = (start + c0) // PIECE
-                    bank = psum.tile([P, PACK, PIECE], F32, name="bank%d" % ((PACK + piece) % 8))
+                for c in range(s[0], s[1], PIECE):
+                    out_banks[c] = psum.tile([P, PACK, PIECE], F32, name="bank%d" % ((PACK + c // PIECE) % BANKS))
+                    cols = slice(c - s[0], c - s[0] + PIECE)
                     for t in range(PACK):
                         nc.tensor.matmul_mx(
-                            out=bank[:, t, :],
-                            lhsT=w2w[:, t, :].bitcast(FP4X4),
-                            lhsT_scale=w2s[:, t, :],
-                            rhs=hid_codes[s][:, c0 : c0 + PIECE].bitcast(FP8X4),
-                            rhs_scale=hid_scales[s][:, c0 : c0 + PIECE],
+                            out=out_banks[c][:, t, :],
+                            lhsT=w2_word_sets[:, t, :].bitcast(FP4X4),
+                            lhsT_scale=w2_scale_sets[:, t, :],
+                            rhs=hid_codes[s][:, cols].bitcast(FP8X4),
+                            rhs_scale=hid_scales[s][:, cols],
                             start=True,
                             stop=True,
                         )
-                    banks[piece] = bank
 
-        def units_of(g):
-            return [u for u in range(len(UNITS)) if group_start[g] <= unit_start[u] < group_start[g] + GROUPS[g]]
+        def store_result(g):
+            for s in stretches[g]:
+                for c in range(s[0], s[1], PIECE):
+                    nc.scalar.copy(result[s][:, :, c - s[0] : c - s[0] + PIECE], out_banks[c][:])
+                nc.sync.dma_start(out_0[:, s[0] : s[1]].rearrange("(p t) r -> p t r", t=PACK), result[s][:])
 
-        def columns(u):
-            return slice(unit_start[u], unit_start[u] + UNITS[u])
-
-        def leave_psum(u):
-            for c0 in range(0, UNITS[u], PIECE):
-                piece = (unit_start[u] + c0) // PIECE
-                if piece in EVICT_ON_VECTOR:
-                    nc.vector.tensor_copy(res[u][:, :, c0 : c0 + PIECE], banks[piece][:])
+        def round_result(g):
+            for s in stretches[g]:
+                if s == stretches[0][-1]:
+                    nc.scalar.copy(rounded[s][:], out_banks[s[0]][:].rearrange("p t n -> p n t"))
                 else:
-                    nc.scalar.copy(res[u][:, :, c0 : c0 + PIECE], banks[piece][:])
-            nc.sync.dma_start(out_0[:, columns(u)].rearrange("(p t) r -> p t r", t=PACK), res[u][:])
+                    nc.vector.tensor_copy(by_words(rounded[s][:]), by_tiles(result[s][:]))
 
-        def round_result(u):
-            if u in ROUND_ON_SCALAR:
-                for c0 in range(0, UNITS[u], PIECE):
-                    bank = banks[(unit_start[u] + c0) // PIECE]
-                    nc.scalar.copy(rounded[u][:, c0 : c0 + PIECE, :], bank[:].rearrange("p t n -> p n t"))
-            else:
-                nc.vector.tensor_copy(words(rounded[u][:]), planes(res[u][:]))
-
-        def quantise_result(u):
-            nc.vector.quantize_mx(
-                out=out_codes[:, columns(u)].bitcast(FP8X4),
-                scales=out_scales[:, columns(u)],
-                in_=rounded[u][:].rearrange("p n t -> p (n t)"),
-            )
-            end = unit_start[u] + UNITS[u]
-            if end in WORD_STORES:
-                cols = slice(WORD_STORES[end], end)
-                nc.sync.dma_start(out_1[0, :, cols, :].rearrange("p n t -> p (n t)").bitcast(I32), out_codes[:, cols])
+        def store_words(g):
+            for s in stretches[g]:
+                nc.vector.quantize_mx(
+                    out=out_codes[:, s[0] : s[1]].bitcast(FP8X4),
+                    scales=out_scales[:, s[0] : s[1]],
+                    in_=rounded[s][:].rearrange("p n t -> p (n t)"),
+                )
+            if g >= last - 1:
+                cols = slice(groups[last][0] if g == last else 0, groups[g][1])
+                nc.sync.dma_start(
+                    out_1[0, :, cols, :].rearrange("p n t -> p (n t)").bitcast(I32), out_codes[:, cols]
+                )
 
         for t in range(PACK):
-            if t in COPY_ON_SCALAR:
+            if t < SCALAR_COPIES:
                 nc.scalar.copy(y[t][:], y_banks[t][:])
             else:
                 nc.vector.tensor_copy(y[t][:], y_banks[t][:])
         for t in range(PACK):
             fetch_first(0, t)
-            if t in ABS_ON_VECTOR:
-                nc.vector.scalar_tensor_tensor(mag[t][:], y[t][:], -1.0, y[t][:], MULT, MAX)
+            if t < VECTOR_ABS:
+                nc.vector.scalar_tensor_tensor(magnitude[t][:], y[t][:], -1.0, y[t][:], MULT, MAX)
             else:
-                nc.scalar.activation(mag[t][:], y[t][:], ACT.Abs)
-            nc.scalar.activation(root[t][:], mag[t][:], ACT.Abs_reciprocal_sqrt, bias=0.7)
+                nc.scalar.activation(magnitude[t][:], y[t][:], ACT.Abs)
+            nc.scalar.activation(root[t][:], magnitude[t][:], ACT.Abs_reciprocal_sqrt, bias=OFFSET)
             fetch_second(0, t)
-            nc.vector.scalar_tensor_tensor(factor[t][:], root[t][:], unit_t[:, t : t + 1], root[t][:], MULT, MULT)
-            if 0 in FUSED:
-                fetch_third(0, t)
+            nc.vector.scalar_tensor_tensor(factor[t][:], root[t][:], unit_rows[:, t : t + 1], root[t][:], MULT, MULT)
+            fetch_third(0, t)
 
-        last = len(GROUPS) - 1
         for g in range(last + 3):
-            if g <= last and not (g == 0 and 0 in FUSED):
+            if 1 <= g <= last:
                 for t in range(PACK):
                     fetch_third(g, t)
             if 1 <= g <= last + 1:
-                for u in units_of(g - 1):
-                    leave_psum(u)
+                store_result(g - 1)
             if g + 1 <= last:
                 for t in range(PACK):
                     fetch_first(g + 1, t)
             if g <= last:
-                make_hid(g)
-            if 2 <= g:
-                for u in units_of(g - 2):
-                    round_result(u)
+                round_hid(g)
+            if g >= 2:
+                round_result(g - 2)
             if g <= last:
                 second_product(g)
-            if 2 <= g:
-                for u in units_of(g - 2):
-                    quantise_result(u)
+            if g >= 2:
+                store_words(g - 2)
             if g + 1 <= last:
                 for t in range(PACK):
                     fetch_second(g + 1, t)
 
-        for q in range(4):
-            (nc.sync if q % 2 == 0 else nc.scalar).dma_start(
+        for q in range(QUADRANTS):
+            queue = nc.sync if q % 2 == 0 else nc.scalar
+            queue.dma_start(
                 out_2[0, 4 * q : 4 * q + 4, :].bitcast(I32), out_scales[32 * q : 32 * q + 4, :].bitcast(I32)
             )

from contextlib import ExitStack

import concourse.mybir as mybir

F32 = mybir.dt.float32
BF16 = mybir.dt.bfloat16
I32 = mybir.dt.int32
U32 = mybir.dt.uint32
U16 = mybir.dt.uint16
U8 = mybir.dt.uint8
FP8X4 = mybir.dt.float8_e4m3fn_x4
FP4X4 = mybir.dt.float4_e2m1fn_x4
ACT = mybir.ActivationFunctionType
MULT = mybir.AluOpType.mult
MAX = mybir.AluOpType.max

P = 128
PACK = 4
PASSES = 2
QUADRANTS = 4
MATERIALS = 1024
PICKED = 512
PIXELS = 1024
BANKS = 8
OFFSET = 0.7

GROUPS = (384, 384, 256)
PIECE = 128
STORE = 256
EARLY_SETS = 2
SCALAR_COPIES = 2
VECTOR_ABS = 1

FLOPS = 2 * 1024 * 512 * 512 + 2 * 512 * 512 * 1024


def tile_picked_yspecmx_rat_po_kernel(
    tc, x_words, x_scales, w1_words, w1_scales, unit, w2_words, w2_scales, offs, e1, e2, e3, out_0, out_1, out_2
):
    nc = tc.nc
    with ExitStack() as ctx:
        keep = ctx.enter_context(tc.tile_pool(name="keep", bufs=1))
        psum = ctx.enter_context(tc.psum_pool(name="psum", bufs=1))

        def sbuf(shape, dtype, name, tag=""):
            return keep.tile(shape, dtype, name=name, tag=tag, align_bytes=64)

        offs_list = keep.tile([P, PICKED // 16], U16, name="offs_list")
        e1_list = keep.tile([P, PIXELS // 16], U16, name="e1_list")
        e2_list = keep.tile([P, PIXELS // 16], U16, name="e2_list")
        e3_list = keep.tile([P, PIXELS // 16], U16, name="e3_list")
        x_word_table = [sbuf([P, MATERIALS], I32, "x_word_table%d" % o) for o in range(PASSES)]
        x_scale_table = sbuf([P, MATERIALS], U8, "x_scale_table")
        w1_words_raw = sbuf([P, PASSES, 2 * PICKED], U8, "w1_words_raw")
        w1_scales_raw = sbuf([P, PASSES, PICKED], U8, "w1_scales_raw")
        w1_word_sets = sbuf([P, PASSES, PACK, 2 * P], U8, "w1_word_sets")
        w1_scales_early = sbuf([P, PASSES, EARLY_SETS, P], U8, "w1_scales_early")
        w2_word_sets = sbuf([P, PACK, 2 * P], U8, "w2_word_sets")
        w2_scale_sets = sbuf([P, PACK, P], U8, "w2_scale_sets")
        picked_words = [sbuf([P, PICKED], U32, "picked_words%d" % o) for o in range(PASSES)]
        picked_scales = [sbuf([P, PICKED], U8, "picked_scales%d" % o) for o in range(PASSES)]
        y = [sbuf([P, PICKED], F32, "y%d" % t) for t in range(PACK)]
        magnitude = [sbuf([P, PICKED], F32, "magnitude%d" % t) for t in range(PACK)]
        root = [sbuf([P, PICKED], F32, "root%d" % t) for t in range(PACK)]
        factor = [sbuf([P, PICKED], F32, "factor%d" % t) for t in range(PACK)]
        out_codes = sbuf([P, PIXELS], I32, "out_codes")
        out_scales = sbuf([P, PIXELS], U8, "out_scales")

        nc.gpsimd.memset(x_scale_table[:].bitcast(I32), 0)
        nc.gpsimd.memset(picked_scales[1][:].bitcast(I32), 0)
        nc.vector.memset(w1_scales_raw[:].rearrange("p o n -> p (o n)").bitcast(I32), 0)

        warm_up = keep.tile([P, 8], F32, name="warm_up")
        nc.vector.memset(warm_up[:, 0:1], 1.0)
        nc.scalar.activation(warm_up[:, 4:5], warm_up[:, 0:1], ACT.Abs_reciprocal_sqrt, bias=OFFSET)

        def load_x_words(o):
            nc.sync.dma_start(x_word_table[o][:], x_words[o].rearrange("p n t -> p (n t)").bitcast(I32))

        nc.sync.dma_start(w1_words_raw[:].bitcast(I32), w1_words.rearrange("o p n -> p o n").bitcast(I32))
        for q in range(QUADRANTS):
            nc.sync.dma_start(
                x_scale_table[32 * q : 32 * q + 4 * PASSES, :].bitcast(I32),
                x_scales[:, 4 * q : 4 * q + 4, :].bitcast(I32),
            )
        nc.sync.dma_start(offs_list[:], offs)
        load_x_words(0)
        for q in range(QUADRANTS):
            nc.sync.dma_start(
                w1_scales_raw[32 * q : 32 * q + 4, :, :].bitcast(I32),
                w1_scales[:, 4 * q : 4 * q + 4, :].rearrange("o r n -> r o n").bitcast(I32),
            )
        load_x_words(1)
        nc.sync.dma_start(e1_list[:], e1)
        nc.sync.dma_start(e2_list[:], e2)
        nc.sync.dma_start(e3_list[:], e3)

        nc.vector.tensor_copy(
            w1_word_sets[:].bitcast(U16), w1_words_raw[:].bitcast(U16).rearrange("p o (m t) -> p o t m", t=PACK)
        )
        nc.vector.tensor_copy(picked_scales[0][:], x_scale_table[:].indirect(offs_list[:]))
        for q in range(QUADRANTS):
            nc.scalar.dma_start(
                picked_scales[1][32 * q : 32 * q + 4, :].bitcast(I32),
                picked_scales[0][32 * q + 4 : 32 * q + 8, :].bitcast(I32),
            )
        w2_scales_raw = sbuf([P, PICKED], U8, "w2_scales_raw", tag="x_scale_table")
        nc.gpsimd.memset(w2_scales_raw[:].bitcast(I32), 0)
        for q in range(QUADRANTS):
            nc.sync.dma_start(
                w2_scales_raw[32 * q : 32 * q + 4, :].bitcast(I32), w2_scales[0, 4 * q : 4 * q + 4, :].bitcast(I32)
            )
        nc.vector.tensor_copy(picked_words[0][:], x_word_table[0][:].bitcast(U32).indirect(offs_list[:]))
        w2_words_raw = sbuf([P, 2 * PICKED], U8, "w2_words_raw", tag="x_word_table0")
        nc.sync.dma_start(w2_words_raw[:].bitcast(I32), w2_words[0].bitcast(I32))
        w1_scales_dealt = w1_scales_raw[:].rearrange("p o (m t) -> p o t m", t=PACK)
        nc.vector.tensor_copy(w1_scales_early[:], w1_scales_dealt[:, :, :EARLY_SETS, :])
        nc.vector.tensor_copy(picked_words[1][:], x_word_table[1][:].bitcast(U32).indirect(offs_list[:]))
        w1_scales_late = sbuf([P, PASSES, PACK - EARLY_SETS, P], U8, "w1_scales_late", tag="x_word_table1")
        nc.vector.tensor_copy(w1_scales_late[:], w1_scales_dealt[:, :, EARLY_SETS:, :])
        unit_rows = sbuf([P, PACK], F32, "unit_rows", tag="w1_scales_raw")
        nc.sync.dma_start(unit_rows[:], unit.rearrange("(p t) c -> p (t c)", t=PACK))

        y_banks = [psum.tile([P, PICKED], F32, name="bank%d" % t) for t in range(PACK)]
        for t in range(PACK):
            for o in range(PASSES):
                nc.tensor.matmul_mx(
                    out=y_banks[t][:],
                    lhsT=w1_word_sets[:, o, t, :].bitcast(FP4X4),
                    lhsT_scale=(
                        w1_scales_early[:, o, t, :] if t < EARLY_SETS else w1_scales_late[:, o, t - EARLY_SETS, :]
                    ),
                    rhs=picked_words[o][:].bitcast(FP8X4),
                    rhs_scale=picked_scales[o][:],
                    start=(o == 0),
                    stop=(o == PASSES - 1),
                )

        nc.vector.tensor_copy(
            w2_word_sets[:].bitcast(U16), w2_words_raw[:].bitcast(U16).rearrange("p (m t) -> p t m", t=PACK)
        )
        nc.vector.tensor_copy(w2_scale_sets[:], w2_scales_raw[:].rearrange("p (m t) -> p t m", t=PACK))

        last = len(GROUPS) - 1
        groups = [(sum(GROUPS[:g]), sum(GROUPS[: g + 1])) for g in range(len(GROUPS))]

        def cut(start, end, step):
            edges = [start] + [c for c in range(start + 1, end) if c % step == 0] + [end]
            return list(zip(edges[:-1], edges[1:]))

        stretches = [cut(start, end, STORE) for start, end in groups[:last]] + [cut(*groups[last], PIECE)]
        spans = [[groups[0]]] + stretches[1:]

        first = [sbuf([P, PACK, n], F32, "first%d" % g) for g, n in enumerate(GROUPS)]
        pair = [sbuf([P, PACK, n], F32, "pair%d" % g) for g, n in enumerate(GROUPS)]
        third = {}
        hid = {s: sbuf([P, s[1] - s[0], PACK], BF16, "hid%d" % s[0]) for group in spans for s in group}
        hid_codes = {s: sbuf([P, s[1] - s[0]], U32, "hid_codes%d" % s[0]) for group in spans for s in group}
        hid_scales = {s: sbuf([P, s[1] - s[0]], U8, "hid_scales%d" % s[0]) for group in spans for s in group}
        result = {s: sbuf([P, PACK, s[1] - s[0]], F32, "result%d" % s[0]) for group in stretches for s in group}
        rounded = {s: sbuf([P, s[1] - s[0], PACK], BF16, "rounded%d" % s[0]) for group in stretches for s in group}
        out_banks = {}

        def entries(index_list, g):
            return index_list[:, groups[g][0] // 16 : groups[g][1] // 16]

        def by_tiles(ap):
            return ap.rearrange("p t (a i) -> p a t i", i=4)

        def by_words(ap):
            return ap.rearrange("p (a i) t -> p a t i", i=4)

        def fetch_first(g, t):
            nc.scalar.activation(first[g][:, t, :], y[t][:].indirect(entries(e1_list, g)), ACT.Copy)

        def fetch_second(g, t):
            nc.vector.tensor_tensor(pair[g][:, t, :], y[t][:].indirect(entries(e2_list, g)), first[g][:, t, :], MULT)

        def fetch_third(g, t):
            if t == 0:
                tag = "hid_codes0" if g == last else "third%d" % g
                third[g] = sbuf([P, PACK, GROUPS[g]], F32, "third%d" % g, tag=tag)
            looked_up = factor[t][:].indirect(entries(e3_list, g))
            if g == 0:
                nc.vector.tensor_tensor(third[g][:, t, :], looked_up, pair[g][:, t, :], MULT)
            else:
                nc.scalar.activation(third[g][:, t, :], looked_up, ACT.Copy)

        def round_hid(g):
            for s in spans[g]:
                if g == 0:
                    nc.vector.tensor_copy(by_words(hid[s][:]), by_tiles(third[g][:]))
                else:
                    cols = slice(s[0] - groups[g][0], s[1] - groups[g][0])
                    nc.vector.tensor_tensor(
                        by_words(hid[s][:]), by_tiles(pair[g][:, :, cols]), by_tiles(third[g][:, :, cols]), MULT
                    )

        def second_product(g):
            for s in spans[g]:
                nc.vector.quantize_mx(
                    out=hid_codes[s][:].bitcast(FP8X4),
                    scales=hid_scales[s][:],
                    in_=hid[s][:].rearrange("p n t -> p (n t)"),
                )
                for c in range(s[0], s[1], PIECE):
                    out_banks[c] = psum.tile([P, PACK, PIECE], F32, name="bank%d" % ((PACK + c // PIECE) % BANKS))
                    cols = slice(c - s[0], c - s[0] + PIECE)
                    for t in range(PACK):
                        nc.tensor.matmul_mx(
                            out=out_banks[c][:, t, :],
                            lhsT=w2_word_sets[:, t, :].bitcast(FP4X4),
                            lhsT_scale=w2_scale_sets[:, t, :],
                            rhs=hid_codes[s][:, cols].bitcast(FP8X4),
                            rhs_scale=hid_scales[s][:, cols],
                            start=True,
                            stop=True,
                        )

        def store_result(g):
            for s in stretches[g]:
                for c in range(s[0], s[1], PIECE):
                    nc.scalar.copy(result[s][:, :, c - s[0] : c - s[0] + PIECE], out_banks[c][:])
                nc.sync.dma_start(out_0[:, s[0] : s[1]].rearrange("(p t) r -> p t r", t=PACK), result[s][:])

        def round_result(g):
            for s in stretches[g]:
                if s == stretches[0][-1]:
                    nc.scalar.copy(rounded[s][:], out_banks[s[0]][:].rearrange("p t n -> p n t"))
                else:
                    nc.vector.tensor_copy(by_words(rounded[s][:]), by_tiles(result[s][:]))

        def store_words(g):
            for s in stretches[g]:
                nc.vector.quantize_mx(
                    out=out_codes[:, s[0] : s[1]].bitcast(FP8X4),
                    scales=out_scales[:, s[0] : s[1]],
                    in_=rounded[s][:].rearrange("p n t -> p (n t)"),
                )
            if g >= last - 1:
                cols = slice(groups[last][0] if g == last else 0, groups[g][1])
                nc.sync.dma_start(
                    out_1[0, :, cols, :].rearrange("p n t -> p (n t)").bitcast(I32), out_codes[:, cols]
                )

        for t in range(PACK):
            if t < SCALAR_COPIES:
                nc.scalar.copy(y[t][:], y_banks[t][:])
            else:
                nc.vector.tensor_copy(y[t][:], y_banks[t][:])
        for t in range(PACK):
            fetch_first(0, t)
            if t < VECTOR_ABS:
                nc.vector.scalar_tensor_tensor(magnitude[t][:], y[t][:], -1.0, y[t][:], MULT, MAX)
            else:
                nc.scalar.activation(magnitude[t][:], y[t][:], ACT.Abs)
            nc.scalar.activation(root[t][:], magnitude[t][:], ACT.Abs_reciprocal_sqrt, bias=OFFSET)
            fetch_second(0, t)
            nc.vector.scalar_tensor_tensor(factor[t][:], root[t][:], unit_rows[:, t : t + 1], root[t][:], MULT, MULT)
            fetch_third(0, t)

        for g in range(last + 3):
            if 1 <= g <= last:
                for t in range(PACK):
                    fetch_third(g, t)
            if 1 <= g <= last + 1:
                store_result(g - 1)
            if g + 1 <= last:
                for t in range(PACK):
                    fetch_first(g + 1, t)
            if g <= last:
                round_hid(g)
            if g >= 2:
                round_result(g - 2)
            if g <= last:
                second_product(g)
            if g >= 2:
                store_words(g - 2)
            if g + 1 <= last:
                for t in range(PACK):
                    fetch_second(g + 1, t)

        for q in range(QUADRANTS):
            queue = nc.sync if q % 2 == 0 else nc.scalar
            queue.dma_start(
                out_2[0, 4 * q : 4 * q + 4, :].bitcast(I32), out_scales[32 * q : 32 * q + 4, :].bitcast(I32)
            )
